import numpy as np
import ml_dtypes


def mxq(x, axis, fmt="e4m3"):
    dtype, down = {"e4m3": (ml_dtypes.float8_e4m3fn, 7), "e5m2": (ml_dtypes.float8_e5m2, 14)}[fmt]
    v = np.moveaxis(np.asarray(x, np.float32).astype(ml_dtypes.bfloat16).astype(np.float64), axis, -1)
    blocks = v.reshape(v.shape[:-1] + (-1, 32))
    amax = np.abs(blocks).max(-1, keepdims=True)
    byte = np.maximum(np.where(amax > 0, np.frexp(amax)[1] - 1 + 127, 0) - down, 1)
    scale = np.exp2(byte - 127.0)
    codes = (blocks / scale).astype(np.float32).astype(dtype).astype(np.float64)
    return np.moveaxis((codes * scale).reshape(v.shape), -1, axis)


WIDE = False


def mx_kscale(k):
    if not WIDE:
        return np.ones(k)
    levels = np.array([10, -10, 5, -5, 0])
    if k % 512:
        return np.exp2(np.random.permutation(np.resize(levels, k // 32))).repeat(32)
    a = np.empty((k // 512, 16))
    for p in range(k // 512):
        a[p, :8] = np.random.permutation(np.resize(levels, 8))
        for g in range(8):
            far = levels[np.abs(levels - a[p, g]) >= 10]
            a[p, g + 8] = far[np.random.randint(len(far))]
    return np.exp2(a.ravel()).repeat(32)


def f64(x):
    return np.asarray(x).astype(np.float64)


def striped(idx):
    return np.tile(np.asarray(idx).reshape(-1, 16).T, (8, 1)).astype(np.uint16)


def unstriped(offs):
    return offs[:16].T.reshape(-1).astype(np.int64)


E2M1 = np.array([0.0, 0.5, 1.0, 1.5, 2.0, 3.0, 4.0, 6.0, -0.0, -0.5, -1.0, -1.5, -2.0, -3.0, -4.0, -6.0])


def pack_weight(w, fmt):
    k, n = w.shape
    w = f64(np.asarray(w, np.float32).astype(ml_dtypes.bfloat16)).reshape(k // 32, 32, n)
    amax = np.abs(w).max(1)
    if fmt == "e4m3":
        byte = np.frexp(amax)[1] - 1 + 127 - 7
    else:
        mant, ex = np.frexp(amax / 6.0)
        byte = np.where(mant > 0.5, ex, ex - 1) + 127
    byte = np.clip(np.where(amax > 0, byte, 1), 1, 254)
    scaled = (w * np.exp2(127.0 - byte)[:, None, :]).reshape(k, n).astype(np.float32)
    by_word = np.ascontiguousarray(scaled.reshape(k // 512, 128, 4, n).transpose(0, 1, 3, 2))
    if fmt == "e4m3":
        words = by_word.astype(ml_dtypes.float8_e4m3fn).view(np.uint8)
    else:
        c = by_word.astype(ml_dtypes.float4_e2m1fn).view(np.uint8) & 0xF
        words = (c[..., 0::2] | (c[..., 1::2] << 4)).reshape(k // 512, 128, 2 * n)
    return np.ascontiguousarray(words), np.ascontiguousarray(byte.astype(np.uint8).reshape(k // 512, 16, n))


def unpack_weight(words, scales, fmt):
    g, _, n = scales.shape
    words = np.ascontiguousarray(words).reshape(g, 128, n, -1)
    if fmt == "e4m3":
        vals = words.view(ml_dtypes.float8_e4m3fn).astype(np.float64)
    else:
        nib = np.empty((g, 128, n, 4), np.uint8)
        nib[..., 0::2] = words & 0xF
        nib[..., 1::2] = words >> 4
        vals = E2M1[nib]
    vals = vals * np.repeat(np.exp2(scales.astype(np.float64) - 127.0), 8, axis=1)[..., None]
    return vals.transpose(0, 1, 3, 2).reshape(g * 512, n)


D, E, T, I, Q = 512, 512, 2048, 512, 128


def setup_inputs():
    n = np.random.standard_normal
    idx = np.random.permutation(T)[:I]
    fd = mx_kscale(D)
    fe = mx_kscale(E)
    keysp = pack_weight(n((D, T)) / fd[:, None], "e4m3")
    valsp = pack_weight(n((E, T)) / fe[:, None], "e4m3")
    return {
        "query": (n((D, Q)) * 0.8 / np.sqrt(D) * fd[:, None]).astype(np.float32),
        "keys_words": keysp[0],
        "keys_scales": keysp[1],
        "bonus": (np.random.uniform(0.5, 2.0, (Q, 1))).astype(np.float32),
        "gout": (n((E, Q)) * 1 / np.sqrt(E) * fe[:, None]).astype(np.float32),
        "vals_words": valsp[0],
        "vals_scales": valsp[1],
        "base": (0.5 * n((Q, T))).astype(np.float32),
        "gq1": (np.random.uniform(0.3, 1.5, (Q, 1))).astype(np.float32),
        "offs": striped(idx),
    }


def reference(query, keys_words, keys_scales, bonus, gout, vals_words, vals_scales, base, gq1, offs):
    idx = unstriped(offs)
    keysu = unpack_weight(keys_words, keys_scales, "e4m3")
    valsu = unpack_weight(vals_words, vals_scales, "e4m3")
    queryq = mxq(f64(query), 0, "e4m3")
    keysidxg = keysu[:, idx]
    a = queryq.T @ keysidxg
    b = a - np.max(a, axis=1, keepdims=True)
    p = np.exp(b)
    z = np.sum(p, axis=1, keepdims=True)
    goutq = mxq(f64(gout), 0, "e4m3")
    valsidxg = valsu[:, idx]
    c0 = goutq.T @ valsidxg
    dz = f64(bonus) / z - np.sum(p * c0, axis=1, keepdims=True) / np.square(z) - f64(bonus) * (-1.0) * np.sum(p * b, axis=1, keepdims=True) / np.square(z)
    dp = 1.0 / z * c0 + f64(bonus) * (-1.0) / z * b + dz
    db = f64(bonus) * (-1.0) / z * p + dp * p
    hdb = db * 512.0 * 2.0 * 512.0
    hdp = hdb * p
    hdz = np.sum(hdp, axis=1, keepdims=True)
    hz = hdz * (-1.0) * np.sum(p * c0, axis=1, keepdims=True) / np.square(np.square(z)) * (-1.0) * z * 2.0 + hdz * (-1.0) * f64(bonus) * (-1.0) * np.sum(p * b, axis=1, keepdims=True) / np.square(np.square(z)) * (-1.0) * z * 2.0 - np.sum(hdb * p, axis=1, keepdims=True) * f64(bonus) * (-1.0) / np.square(z) - np.sum(hdp * c0, axis=1, keepdims=True) / np.square(z) - np.sum(hdp * b, axis=1, keepdims=True) * f64(bonus) * (-1.0) / np.square(z) - hdz * f64(bonus) / np.square(z)
    hp = hdb * f64(bonus) * (-1.0) / z + hdb * dp + hdz * (-1.0) / np.square(z) * c0 + hdz * (-1.0) / np.square(z) * f64(bonus) * (-1.0) * b + hz
    hb = hdp * f64(bonus) * (-1.0) / z + hdz * (-1.0) / np.square(z) * f64(bonus) * (-1.0) * p + hp * p
    gs = hb * f64(gq1)
    gf = np.zeros((Q, T))
    gf[:, idx] = gs
    y = f64(base) + gf
    return y

@@ -1,0 +1,172 @@
+from contextlib import ExitStack
+
+import concourse.mybir as mybir
+
+D, E, T, I, Q = 512, 512, 2048, 512, 128
+FLOPS = 2 * Q * I * (D + E)
+
+F32 = mybir.dt.float32
+BF16 = mybir.dt.bfloat16
+I32 = mybir.dt.int32
+U32 = mybir.dt.uint32
+U16 = mybir.dt.uint16
+U8 = mybir.dt.uint8
+FP8X4 = mybir.dt.float8_e4m3fn_x4
+ALU = mybir.AluOpType
+ACT = mybir.ActivationFunctionType
+
+P = 128
+PACK = 4
+HALF = I // 2
+VAL_ROW = 4
+STORE_COLS = (256, 256, 512, 512, 512)
+
+
+def tile_attend_gpentropybonus_kernel(tc, query, keys_words, keys_scales, bonus, gout, vals_words, vals_scales, base, gq1, offs, out):
+    nc = tc.nc
+    with ExitStack() as ctx:
+        pool = ctx.enter_context(tc.tile_pool(name="pool", bufs=1))
+        psum = ctx.enter_context(tc.psum_pool(name="psum", bufs=1))
+
+        def col(name):
+            return pool.tile([P, 1], F32, name=name)
+
+        def row(name):
+            return pool.tile([P, I], F32, name=name)
+
+        offsets = pool.tile([P, I // 16], U16, name="offsets")
+        nc.sync.dma_start(offsets[:], offs)
+
+        key_bytes = pool.tile([P, T], U8, name="key_bytes")
+        val_bytes = pool.tile([P, T], U8, name="val_bytes")
+        nc.vector.memset(key_bytes[:].bitcast(I32), 0)
+        nc.vector.memset(val_bytes[:].bitcast(I32), 0)
+
+        def load_scale_rows(queue, tile, scales, first):
+            rows = scales[0].rearrange("(a j) t -> j a t", j=4)
+            for j in range(4):
+                queue.dma_start(tile[first + j : P : 32, :].bitcast(I32), rows[j].bitcast(I32))
+
+        load_scale_rows(nc.sync, key_bytes, keys_scales, 0)
+        query_raw = pool.tile([P, PACK, Q], F32, name="query_raw")
+        nc.sync.dma_start(query_raw[:], query.rearrange("(p j) q -> p j q", j=PACK))
+        key_words = pool.tile([P, T], U32, name="key_words")
+        nc.sync.dma_start(key_words[:].bitcast(I32), keys_words[0].rearrange("p n t -> p (n t)").bitcast(I32))
+        load_scale_rows(nc.sync, val_bytes, vals_scales, VAL_ROW)
+        gout_raw = pool.tile([P, PACK, Q], F32, name="gout_raw")
+        nc.sync.dma_start(gout_raw[:], gout.rearrange("(p j) q -> p j q", j=PACK))
+        val_words = pool.tile([P, T], U32, name="val_words")
+        nc.sync.dma_start(val_words[:].bitcast(I32), vals_words[0].rearrange("p n t -> p (n t)").bitcast(I32))
+        beta = col("beta")
+        nc.sync.dma_start(beta[:], bonus)
+        factor = col("factor")
+        nc.sync.dma_start(factor[:], gq1)
+        base_sb = pool.tile([P, T], F32, name="base_sb")
+        nc.sync.dma_start(base_sb[:], base)
+
+        window = pool.tile([P, T], F32, name="window")
+        nc.vector.memset(window[:], 0.0)
+
+        def quantise(raw, name):
+            grouped = pool.tile([P, Q, PACK], BF16, name=name + "_grouped", align_bytes=64)
+            nc.scalar.copy(grouped[:], raw[:].rearrange("p j q -> p q j"))
+            codes = pool.tile([P, Q], U32, name=name + "_codes", align_bytes=64)
+            scales = pool.tile([P, Q], U8, name=name + "_scales", align_bytes=64)
+            nc.vector.quantize_mx(out=codes[:].bitcast(FP8X4), scales=scales[:], in_=grouped[:].rearrange("p q j -> p (q j)"))
+            return codes, scales
+
+        def gather_bytes(tile, name):
+            picked = pool.tile([P, I], U8, name=name, align_bytes=64)
+            nc.vector.tensor_copy(picked[:], tile[:].indirect(offsets[:]))
+            return picked
+
+        def product(words, picked_bytes, first, codes, scales, name):
+            banks = []
+            for h in range(2):
+                picked = pool.tile([P, HALF], U32, name=name + "_picked%d" % h, align_bytes=64)
+                nc.vector.tensor_copy(picked[:], words[:].indirect(offsets[:, h * HALF // 16 : (h + 1) * HALF // 16]))
+                bank = psum.tile([P, HALF], F32, name=name + "_bank%d" % h)
+                nc.tensor.matmul_mx(
+                    out=bank[:],
+                    lhsT=codes[:].bitcast(FP8X4),
+                    lhsT_scale=scales[:],
+                    rhs=picked[:].bitcast(FP8X4),
+                    rhs_scale=picked_bytes[first:P, h * HALF : (h + 1) * HALF],
+                    start=True,
+                    stop=True,
+                )
+                banks.append(bank)
+            return banks
+
+        halves = [slice(0, HALF), slice(HALF, I)]
+
+        key_picked_bytes = gather_bytes(key_bytes, "key_picked_bytes")
+        query_codes, query_scales = quantise(query_raw, "query")
+        score_banks = product(key_words, key_picked_bytes, 0, query_codes, query_scales, "score")
+
+        neg_a = row("neg_a")
+        neg_max_first = col("neg_max_first")
+        neg_max = col("neg_max")
+        nc.vector.tensor_scalar(neg_a[:, halves[0]], score_banks[0][:], -1.0, None, ALU.mult, ALU.min, accum_out=neg_max_first[:])
+        nc.vector.tensor_scalar(neg_a[:, halves[1]], score_banks[1][:], -1.0, neg_max_first[:], ALU.mult, ALU.min, accum_out=neg_max[:])
+        p = row("p")
+        z = col("z")
+        nc.scalar.activation(p[:], neg_a[:], ACT.Exp, bias=neg_max[:], scale=-1.0, accum_out=z[:])
+        p_sq = row("p_sq")
+        nc.scalar.activation(p_sq[:], p[:], ACT.Square)
+
+        half_beta = col("half_beta")
+        nc.gpsimd.tensor_scalar(half_beta[:], beta[:], 0.5, 0.0, ALU.mult, ALU.add)
+        half_beta_sq = col("half_beta_sq")
+        nc.gpsimd.tensor_tensor(half_beta_sq[:], half_beta[:], half_beta[:], ALU.mult)
+        amp = col("amp")
+        nc.gpsimd.tensor_scalar(amp[:], factor[:], 2.0 * 512.0 * 512.0, 0.0, ALU.mult, ALU.add)
+
+        val_picked_bytes = gather_bytes(val_bytes, "val_picked_bytes")
+        gout_codes, gout_scales = quantise(gout_raw, "gout")
+        c0_banks = product(val_words, val_picked_bytes, VAL_ROW, gout_codes, gout_scales, "c0")
+
+        inv_z = col("inv_z")
+        nc.vector.reciprocal(inv_z[:], z[:])
+        neg_inv_z = col("neg_inv_z")
+        nc.vector.tensor_scalar(neg_inv_z[:], inv_z[:], -1.0, None, ALU.mult)
+        amp_inv_z_sq = col("amp_inv_z_sq")
+        nc.vector.scalar_tensor_tensor(amp_inv_z_sq[:], inv_z[:], amp[:], inv_z[:], ALU.mult, ALU.mult)
+        neg_s = row("neg_s")
+        nc.scalar.activation(neg_s[:], p[:], ACT.Copy, scale=neg_inv_z[:])
+        s_sq = row("s_sq")
+        sum_s_sq = col("sum_s_sq")
+        nc.scalar.activation(s_sq[:], p_sq[:], ACT.Copy, scale=amp_inv_z_sq[:], accum_out=sum_s_sq[:])
+
+        u = row("u")
+        for h in range(2):
+            nc.vector.scalar_tensor_tensor(u[:, halves[h]], neg_a[:, halves[h]], beta[:], c0_banks[h][:], ALU.mult, ALU.add)
+        t = row("t")
+        neg_mean = col("neg_mean")
+        nc.vector.scalar_tensor_tensor(t[:], u[:], half_beta[:], neg_s[:], ALU.add, ALU.mult, accum_out=neg_mean[:])
+        centred_sq = row("centred_sq")
+        nc.scalar.activation(centred_sq[:], u[:], ACT.Square, bias=neg_mean[:], scale=1.0)
+        x = row("x")
+        moment = col("moment")
+        nc.vector.scalar_tensor_tensor(x[:], u[:], half_beta[:], s_sq[:], ALU.add, ALU.mult, accum_out=moment[:])
+        g_sum = col("g_sum")
+        nc.vector.tensor_scalar(g_sum[:], sum_s_sq[:], neg_mean[:], moment[:], ALU.mult, ALU.add)
+        gt = row("gt")
+        nc.scalar.activation(gt[:], t[:], ACT.Copy, scale=g_sum[:])
+        y = row("y")
+        y_sum = col("y_sum")
+        nc.vector.scalar_tensor_tensor(y[:], centred_sq[:], half_beta_sq[:], s_sq[:], ALU.subtract, ALU.mult, accum_out=y_sum[:])
+        c = col("c")
+        nc.vector.tensor_scalar(c[:], g_sum[:], neg_mean[:], y_sum[:], ALU.mult, ALU.add)
+        f = row("f")
+        nc.vector.scalar_tensor_tensor(f[:], neg_s[:], c[:], y[:], ALU.mult, ALU.add)
+        nc.vector.tensor_tensor(window[:].indirect(offsets[:]), f[:], gt[:], ALU.add)
+
+        result = pool.tile([P, T], F32, name="result")
+        start = 0
+        for n, width in enumerate(STORE_COLS):
+            cols = slice(start, start + width)
+            nc.vector.tensor_tensor(result[:, cols], window[:, cols], base_sb[:, cols], ALU.add)
+            queue = nc.sync if n % 2 == 0 else nc.scalar
+            queue.dma_start(out[:, cols], result[:, cols])
+            start = start + width

@@ -1,3 +1,4 @@
+import math
 from contextlib import ExitStack
 
 import concourse.mybir as mybir
@@ -18,8 +19,7 @@ ACT = mybir.ActivationFunctionType
 P = 128
 PACK = 4
 HALF = I // 2
-VAL_ROW = 4
-STORE_COLS = (256, 256, 512, 512, 512)
+STORE_COLS = (256, 512, 512, 512, 256)
 
 
 def tile_attend_gpentropybonus_kernel(tc, query, keys_words, keys_scales, bonus, gout, vals_words, vals_scales, base, gq1, offs, out):
@@ -34,41 +34,40 @@ def tile_attend_gpentropybonus_kernel(tc, query, keys_words, keys_scales, bonus,
         def row(name):
             return pool.tile([P, I], F32, name=name)
 
+        halves = [slice(0, HALF), slice(HALF, I)]
+
         offsets = pool.tile([P, I // 16], U16, name="offsets")
         nc.sync.dma_start(offsets[:], offs)
 
-        key_bytes = pool.tile([P, T], U8, name="key_bytes")
         val_bytes = pool.tile([P, T], U8, name="val_bytes")
-        nc.vector.memset(key_bytes[:].bitcast(I32), 0)
+        key_bytes = pool.tile([P, T], U8, name="key_bytes")
+        val_plane = pool.tile([P, I], U8, name="val_plane", align_bytes=64)
         nc.vector.memset(val_bytes[:].bitcast(I32), 0)
+        nc.vector.memset(key_bytes[:].bitcast(I32), 0)
+        nc.vector.memset(val_plane[:].bitcast(I32), 0)
 
-        def load_scale_rows(queue, tile, scales, first):
-            rows = scales[0].rearrange("(a j) t -> j a t", j=4)
-            for j in range(4):
-                queue.dma_start(tile[first + j : P : 32, :].bitcast(I32), rows[j].bitcast(I32))
-
-        load_scale_rows(nc.sync, key_bytes, keys_scales, 0)
+        nc.sync.dma_start(val_bytes[0:P:8, :].bitcast(I32), vals_scales[0].bitcast(I32))
         query_raw = pool.tile([P, PACK, Q], F32, name="query_raw")
         nc.sync.dma_start(query_raw[:], query.rearrange("(p j) q -> p j q", j=PACK))
-        key_words = pool.tile([P, T], U32, name="key_words")
+        key_rows = keys_scales[0].rearrange("(a j) t -> j a t", j=4)
+        for j in range(4):
+            nc.sync.dma_start(key_bytes[j:P:32, :].bitcast(I32), key_rows[j].bitcast(I32))
+        key_words = pool.tile([P, T], U32, name="key_words", tag="key_words")
         nc.sync.dma_start(key_words[:].bitcast(I32), keys_words[0].rearrange("p n t -> p (n t)").bitcast(I32))
-        load_scale_rows(nc.sync, val_bytes, vals_scales, VAL_ROW)
-        gout_raw = pool.tile([P, PACK, Q], F32, name="gout_raw")
+        gout_raw = pool.tile([P, PACK, Q], F32, name="gout_raw", tag="gout_raw")
         nc.sync.dma_start(gout_raw[:], gout.rearrange("(p j) q -> p j q", j=PACK))
-        val_words = pool.tile([P, T], U32, name="val_words")
+        val_words = pool.tile([P, T], U32, name="val_words", tag="val_words")
         nc.sync.dma_start(val_words[:].bitcast(I32), vals_words[0].rearrange("p n t -> p (n t)").bitcast(I32))
         beta = col("beta")
         nc.sync.dma_start(beta[:], bonus)
         factor = col("factor")
         nc.sync.dma_start(factor[:], gq1)
-        base_sb = pool.tile([P, T], F32, name="base_sb")
-        nc.sync.dma_start(base_sb[:], base)
 
         window = pool.tile([P, T], F32, name="window")
         nc.vector.memset(window[:], 0.0)
 
         def quantise(raw, name):
-            grouped = pool.tile([P, Q, PACK], BF16, name=name + "_grouped", align_bytes=64)
+            grouped = pool.tile([P, Q, PACK], BF16, name=name + "_grouped", tag=name + "_grouped", align_bytes=64)
             nc.scalar.copy(grouped[:], raw[:].rearrange("p j q -> p q j"))
             codes = pool.tile([P, Q], U32, name=name + "_codes", align_bytes=64)
             scales = pool.tile([P, Q], U8, name=name + "_scales", align_bytes=64)
@@ -80,63 +79,59 @@ def tile_attend_gpentropybonus_kernel(tc, query, keys_words, keys_scales, bonus,
             nc.vector.tensor_copy(picked[:], tile[:].indirect(offsets[:]))
             return picked
 
-        def product(words, picked_bytes, first, codes, scales, name):
-            banks = []
-            for h in range(2):
-                picked = pool.tile([P, HALF], U32, name=name + "_picked%d" % h, align_bytes=64)
-                nc.vector.tensor_copy(picked[:], words[:].indirect(offsets[:, h * HALF // 16 : (h + 1) * HALF // 16]))
-                bank = psum.tile([P, HALF], F32, name=name + "_bank%d" % h)
-                nc.tensor.matmul_mx(
-                    out=bank[:],
-                    lhsT=codes[:].bitcast(FP8X4),
-                    lhsT_scale=scales[:],
-                    rhs=picked[:].bitcast(FP8X4),
-                    rhs_scale=picked_bytes[first:P, h * HALF : (h + 1) * HALF],
-                    start=True,
-                    stop=True,
-                )
-                banks.append(bank)
-            return banks
+        def half_product(h, words, plane, codes, scales, dest, name, tag):
+            picked = pool.tile([P, HALF], U32, name=name, tag=tag, align_bytes=64)
+            nc.vector.tensor_copy(picked[:], words[:].indirect(offsets[:, h * HALF // 16 : (h + 1) * HALF // 16]))
+            nc.tensor.matmul_mx(
+                out=dest,
+                lhsT=codes[:].bitcast(FP8X4),
+                lhsT_scale=scales[:],
+                rhs=picked[:].bitcast(FP8X4),
+                rhs_scale=plane[:, halves[h]],
+                start=True,
+                stop=True,
+            )
 
-        halves = [slice(0, HALF), slice(HALF, I)]
-
-        key_picked_bytes = gather_bytes(key_bytes, "key_picked_bytes")
+        val_picked_bytes = gather_bytes(val_bytes, "val_picked_bytes")
+        for j in range(4):
+            nc.scalar.dma_start(val_plane[j:P:32, :].bitcast(I32), val_picked_bytes[8 * j : P : 32, :].bitcast(I32))
+        key_plane = gather_bytes(key_bytes, "key_plane")
         query_codes, query_scales = quantise(query_raw, "query")
-        score_banks = product(key_words, key_picked_bytes, 0, query_codes, query_scales, "score")
+        score_bank = psum.tile([P, I], F32, name="score_bank")
+        for h in range(2):
+            half_product(h, key_words, key_plane, query_codes, query_scales, score_bank[:, halves[h]], "key_picked%d" % h, "key_picked%d" % h)
+        base_sb = pool.tile([P, T], F32, name="base_sb", tag="key_words")
+        nc.sync.dma_start(base_sb[:], base)
 
+        gout_codes, gout_scales = quantise(gout_raw, "gout")
         neg_a = row("neg_a")
-        neg_max_first = col("neg_max_first")
         neg_max = col("neg_max")
-        nc.vector.tensor_scalar(neg_a[:, halves[0]], score_banks[0][:], -1.0, None, ALU.mult, ALU.min, accum_out=neg_max_first[:])
-        nc.vector.tensor_scalar(neg_a[:, halves[1]], score_banks[1][:], -1.0, neg_max_first[:], ALU.mult, ALU.min, accum_out=neg_max[:])
-        p = row("p")
+        nc.vector.tensor_scalar(neg_a[:], score_bank[:], -1.0, None, ALU.mult, ALU.min, accum_out=neg_max[:])
+        p = pool.tile([P, I], F32, name="p", tag="gout_raw")
         z = col("z")
         nc.scalar.activation(p[:], neg_a[:], ACT.Exp, bias=neg_max[:], scale=-1.0, accum_out=z[:])
         p_sq = row("p_sq")
-        nc.scalar.activation(p_sq[:], p[:], ACT.Square)
-
+        nc.scalar.activation(p_sq[:], p[:], ACT.Square, scale=512.0 * math.sqrt(2.0))
         half_beta = col("half_beta")
-        nc.gpsimd.tensor_scalar(half_beta[:], beta[:], 0.5, 0.0, ALU.mult, ALU.add)
+        nc.scalar.activation(half_beta[:], beta[:], ACT.Copy, scale=0.5)
         half_beta_sq = col("half_beta_sq")
-        nc.gpsimd.tensor_tensor(half_beta_sq[:], half_beta[:], half_beta[:], ALU.mult)
-        amp = col("amp")
-        nc.gpsimd.tensor_scalar(amp[:], factor[:], 2.0 * 512.0 * 512.0, 0.0, ALU.mult, ALU.add)
+        nc.scalar.activation(half_beta_sq[:], beta[:], ACT.Square, scale=0.5)
 
-        val_picked_bytes = gather_bytes(val_bytes, "val_picked_bytes")
-        gout_codes, gout_scales = quantise(gout_raw, "gout")
-        c0_banks = product(val_words, val_picked_bytes, VAL_ROW, gout_codes, gout_scales, "c0")
+        c0_banks = [psum.tile([P, HALF], F32, name="c0_bank%d" % h) for h in range(2)]
+        for h, tag in enumerate(("gout_grouped", "val_picked1")):
+            half_product(h, val_words, val_plane, gout_codes, gout_scales, c0_banks[h][:], "val_picked%d" % h, tag)
 
-        inv_z = col("inv_z")
+        inv_z = pool.tile([P, 1], F32, name="inv_z", tag="val_words")
         nc.vector.reciprocal(inv_z[:], z[:])
         neg_inv_z = col("neg_inv_z")
         nc.vector.tensor_scalar(neg_inv_z[:], inv_z[:], -1.0, None, ALU.mult)
-        amp_inv_z_sq = col("amp_inv_z_sq")
-        nc.vector.scalar_tensor_tensor(amp_inv_z_sq[:], inv_z[:], amp[:], inv_z[:], ALU.mult, ALU.mult)
+        factor_inv_z_sq = col("factor_inv_z_sq")
+        nc.vector.scalar_tensor_tensor(factor_inv_z_sq[:], inv_z[:], factor[:], inv_z[:], ALU.mult, ALU.mult)
         neg_s = row("neg_s")
         nc.scalar.activation(neg_s[:], p[:], ACT.Copy, scale=neg_inv_z[:])
         s_sq = row("s_sq")
         sum_s_sq = col("sum_s_sq")
-        nc.scalar.activation(s_sq[:], p_sq[:], ACT.Copy, scale=amp_inv_z_sq[:], accum_out=sum_s_sq[:])
+        nc.scalar.activation(s_sq[:], p_sq[:], ACT.Copy, scale=factor_inv_z_sq[:], accum_out=sum_s_sq[:])
 
         u = row("u")
         for h in range(2):
@@ -151,16 +146,16 @@ def tile_attend_gpentropybonus_kernel(tc, query, keys_words, keys_scales, bonus,
         nc.vector.scalar_tensor_tensor(x[:], u[:], half_beta[:], s_sq[:], ALU.add, ALU.mult, accum_out=moment[:])
         g_sum = col("g_sum")
         nc.vector.tensor_scalar(g_sum[:], sum_s_sq[:], neg_mean[:], moment[:], ALU.mult, ALU.add)
-        gt = row("gt")
-        nc.scalar.activation(gt[:], t[:], ACT.Copy, scale=g_sum[:])
         y = row("y")
         y_sum = col("y_sum")
         nc.vector.scalar_tensor_tensor(y[:], centred_sq[:], half_beta_sq[:], s_sq[:], ALU.subtract, ALU.mult, accum_out=y_sum[:])
         c = col("c")
         nc.vector.tensor_scalar(c[:], g_sum[:], neg_mean[:], y_sum[:], ALU.mult, ALU.add)
+        cs = row("cs")
+        nc.scalar.activation(cs[:], neg_s[:], ACT.Copy, scale=c[:])
         f = row("f")
-        nc.vector.scalar_tensor_tensor(f[:], neg_s[:], c[:], y[:], ALU.mult, ALU.add)
-        nc.vector.tensor_tensor(window[:].indirect(offsets[:]), f[:], gt[:], ALU.add)
+        nc.vector.scalar_tensor_tensor(f[:], t[:], g_sum[:], y[:], ALU.mult, ALU.add)
+        nc.vector.tensor_tensor(window[:].indirect(offsets[:]), f[:], cs[:], ALU.add)
 
         result = pool.tile([P, T], F32, name="result")
         start = 0

@@ -123,12 +123,10 @@ def tile_attend_gpentropybonus_kernel(tc, query, keys_words, keys_scales, bonus,
 
         inv_z = pool.tile([P, 1], F32, name="inv_z", tag="val_words")
         nc.vector.reciprocal(inv_z[:], z[:])
-        neg_inv_z = col("neg_inv_z")
-        nc.vector.tensor_scalar(neg_inv_z[:], inv_z[:], -1.0, None, ALU.mult)
         factor_inv_z_sq = col("factor_inv_z_sq")
         nc.vector.scalar_tensor_tensor(factor_inv_z_sq[:], inv_z[:], factor[:], inv_z[:], ALU.mult, ALU.mult)
-        neg_s = row("neg_s")
-        nc.scalar.activation(neg_s[:], p[:], ACT.Copy, scale=neg_inv_z[:])
+        s = row("s")
+        nc.scalar.activation(s[:], p[:], ACT.Copy, scale=inv_z[:])
         s_sq = row("s_sq")
         sum_s_sq = col("sum_s_sq")
         nc.scalar.activation(s_sq[:], p_sq[:], ACT.Copy, scale=factor_inv_z_sq[:], accum_out=sum_s_sq[:])
@@ -137,24 +135,26 @@ def tile_attend_gpentropybonus_kernel(tc, query, keys_words, keys_scales, bonus,
         for h in range(2):
             nc.vector.scalar_tensor_tensor(u[:, halves[h]], neg_a[:, halves[h]], beta[:], c0_banks[h][:], ALU.mult, ALU.add)
         t = row("t")
-        neg_mean = col("neg_mean")
-        nc.vector.scalar_tensor_tensor(t[:], u[:], half_beta[:], neg_s[:], ALU.add, ALU.mult, accum_out=neg_mean[:])
+        mean = col("mean")
+        nc.vector.scalar_tensor_tensor(t[:], u[:], half_beta[:], s[:], ALU.add, ALU.mult, accum_out=mean[:])
         centred_sq = row("centred_sq")
-        nc.scalar.activation(centred_sq[:], u[:], ACT.Square, bias=neg_mean[:], scale=1.0)
+        nc.scalar.activation(centred_sq[:], u[:], ACT.Square, bias=mean[:], scale=-1.0)
         x = row("x")
         moment = col("moment")
         nc.vector.scalar_tensor_tensor(x[:], u[:], half_beta[:], s_sq[:], ALU.add, ALU.mult, accum_out=moment[:])
-        g_sum = col("g_sum")
-        nc.vector.tensor_scalar(g_sum[:], sum_s_sq[:], neg_mean[:], moment[:], ALU.mult, ALU.add)
+        neg_g = col("neg_g")
+        nc.vector.tensor_scalar(neg_g[:], sum_s_sq[:], mean[:], moment[:], ALU.mult, ALU.subtract)
+        neg_g_mean = col("neg_g_mean")
+        nc.scalar.activation(neg_g_mean[:], neg_g[:], ACT.Copy, scale=mean[:])
         y = row("y")
         y_sum = col("y_sum")
         nc.vector.scalar_tensor_tensor(y[:], centred_sq[:], half_beta_sq[:], s_sq[:], ALU.subtract, ALU.mult, accum_out=y_sum[:])
         c = col("c")
-        nc.vector.tensor_scalar(c[:], g_sum[:], neg_mean[:], y_sum[:], ALU.mult, ALU.add)
+        nc.vector.tensor_scalar(c[:], y_sum[:], -1.0, neg_g_mean[:], ALU.mult, ALU.subtract)
         cs = row("cs")
-        nc.scalar.activation(cs[:], neg_s[:], ACT.Copy, scale=c[:])
+        nc.scalar.activation(cs[:], s[:], ACT.Copy, scale=c[:])
         f = row("f")
-        nc.vector.scalar_tensor_tensor(f[:], t[:], g_sum[:], y[:], ALU.mult, ALU.add)
+        nc.vector.scalar_tensor_tensor(f[:], t[:], neg_g[:], y[:], ALU.mult, ALU.add)
         nc.vector.tensor_tensor(window[:].indirect(offsets[:]), f[:], cs[:], ALU.add)
 
         result = pool.tile([P, T], F32, name="result")

import math
from contextlib import ExitStack

import concourse.mybir as mybir

D, E, T, I, Q = 512, 512, 2048, 512, 128
FLOPS = 2 * Q * I * (D + E)

F32 = mybir.dt.float32
BF16 = mybir.dt.bfloat16
I32 = mybir.dt.int32
U32 = mybir.dt.uint32
U16 = mybir.dt.uint16
U8 = mybir.dt.uint8
FP8X4 = mybir.dt.float8_e4m3fn_x4
ALU = mybir.AluOpType
ACT = mybir.ActivationFunctionType

P = 128
PACK = 4
HALF = I // 2
STORE_COLS = (256, 512, 512, 512, 256)


def tile_attend_gpentropybonus_kernel(tc, query, keys_words, keys_scales, bonus, gout, vals_words, vals_scales, base, gq1, offs, out):
    nc = tc.nc
    with ExitStack() as ctx:
        pool = ctx.enter_context(tc.tile_pool(name="pool", bufs=1))
        psum = ctx.enter_context(tc.psum_pool(name="psum", bufs=1))

        def col(name):
            return pool.tile([P, 1], F32, name=name)

        def row(name):
            return pool.tile([P, I], F32, name=name)

        halves = [slice(0, HALF), slice(HALF, I)]

        offsets = pool.tile([P, I // 16], U16, name="offsets")
        nc.sync.dma_start(offsets[:], offs)

        val_bytes = pool.tile([P, T], U8, name="val_bytes")
        key_bytes = pool.tile([P, T], U8, name="key_bytes")
        val_plane = pool.tile([P, I], U8, name="val_plane", align_bytes=64)
        nc.vector.memset(val_bytes[:].bitcast(I32), 0)
        nc.vector.memset(key_bytes[:].bitcast(I32), 0)
        nc.vector.memset(val_plane[:].bitcast(I32), 0)

        nc.sync.dma_start(val_bytes[0:P:8, :].bitcast(I32), vals_scales[0].bitcast(I32))
        query_raw = pool.tile([P, PACK, Q], F32, name="query_raw")
        nc.sync.dma_start(query_raw[:], query.rearrange("(p j) q -> p j q", j=PACK))
        key_rows = keys_scales[0].rearrange("(a j) t -> j a t", j=4)
        for j in range(4):
            nc.sync.dma_start(key_bytes[j:P:32, :].bitcast(I32), key_rows[j].bitcast(I32))
        key_words = pool.tile([P, T], U32, name="key_words", tag="key_words")
        nc.sync.dma_start(key_words[:].bitcast(I32), keys_words[0].rearrange("p n t -> p (n t)").bitcast(I32))
        gout_raw = pool.tile([P, PACK, Q], F32, name="gout_raw", tag="gout_raw")
        nc.sync.dma_start(gout_raw[:], gout.rearrange("(p j) q -> p j q", j=PACK))
        val_words = pool.tile([P, T], U32, name="val_words", tag="val_words")
        nc.sync.dma_start(val_words[:].bitcast(I32), vals_words[0].rearrange("p n t -> p (n t)").bitcast(I32))
        beta = col("beta")
        nc.sync.dma_start(beta[:], bonus)
        factor = col("factor")
        nc.sync.dma_start(factor[:], gq1)

        window = pool.tile([P, T], F32, name="window")
        nc.vector.memset(window[:], 0.0)

        def quantise(raw, name):
            grouped = pool.tile([P, Q, PACK], BF16, name=name + "_grouped", tag=name + "_grouped", align_bytes=64)
            nc.scalar.copy(grouped[:], raw[:].rearrange("p j q -> p q j"))
            codes = pool.tile([P, Q], U32, name=name + "_codes", align_bytes=64)
            scales = pool.tile([P, Q], U8, name=name + "_scales", align_bytes=64)
            nc.vector.quantize_mx(out=codes[:].bitcast(FP8X4), scales=scales[:], in_=grouped[:].rearrange("p q j -> p (q j)"))
            return codes, scales

        def gather_bytes(tile, name):
            picked = pool.tile([P, I], U8, name=name, align_bytes=64)
            nc.vector.tensor_copy(picked[:], tile[:].indirect(offsets[:]))
            return picked

        def half_product(h, words, plane, codes, scales, dest, name, tag):
            picked = pool.tile([P, HALF], U32, name=name, tag=tag, align_bytes=64)
            nc.vector.tensor_copy(picked[:], words[:].indirect(offsets[:, h * HALF // 16 : (h + 1) * HALF // 16]))
            nc.tensor.matmul_mx(
                out=dest,
                lhsT=codes[:].bitcast(FP8X4),
                lhsT_scale=scales[:],
                rhs=picked[:].bitcast(FP8X4),
                rhs_scale=plane[:, halves[h]],
                start=True,
                stop=True,
            )

        val_picked_bytes = gather_bytes(val_bytes, "val_picked_bytes")
        for j in range(4):
            nc.scalar.dma_start(val_plane[j:P:32, :].bitcast(I32), val_picked_bytes[8 * j : P : 32, :].bitcast(I32))
        key_plane = gather_bytes(key_bytes, "key_plane")
        query_codes, query_scales = quantise(query_raw, "query")
        score_bank = psum.tile([P, I], F32, name="score_bank")
        for h in range(2):
            half_product(h, key_words, key_plane, query_codes, query_scales, score_bank[:, halves[h]], "key_picked%d" % h, "key_picked%d" % h)
        base_sb = pool.tile([P, T], F32, name="base_sb", tag="key_words")
        nc.sync.dma_start(base_sb[:], base)

        gout_codes, gout_scales = quantise(gout_raw, "gout")
        neg_a = row("neg_a")
        neg_max = col("neg_max")
        nc.vector.tensor_scalar(neg_a[:], score_bank[:], -1.0, None, ALU.mult, ALU.min, accum_out=neg_max[:])
        p = pool.tile([P, I], F32, name="p", tag="gout_raw")
        z = col("z")
        nc.scalar.activation(p[:], neg_a[:], ACT.Exp, bias=neg_max[:], scale=-1.0, accum_out=z[:])
        p_sq = row("p_sq")
        nc.scalar.activation(p_sq[:], p[:], ACT.Square, scale=512.0 * math.sqrt(2.0))
        half_beta = col("half_beta")
        nc.scalar.activation(half_beta[:], beta[:], ACT.Copy, scale=0.5)
        half_beta_sq = col("half_beta_sq")
        nc.scalar.activation(half_beta_sq[:], beta[:], ACT.Square, scale=0.5)

        c0_banks = [psum.tile([P, HALF], F32, name="c0_bank%d" % h) for h in range(2)]
        for h, tag in enumerate(("gout_grouped", "val_picked1")):
            half_product(h, val_words, val_plane, gout_codes, gout_scales, c0_banks[h][:], "val_picked%d" % h, tag)

        inv_z = pool.tile([P, 1], F32, name="inv_z", tag="val_words")
        nc.vector.reciprocal(inv_z[:], z[:])
        factor_inv_z_sq = col("factor_inv_z_sq")
        nc.vector.scalar_tensor_tensor(factor_inv_z_sq[:], inv_z[:], factor[:], inv_z[:], ALU.mult, ALU.mult)
        s = row("s")
        nc.scalar.activation(s[:], p[:], ACT.Copy, scale=inv_z[:])
        s_sq = row("s_sq")
        sum_s_sq = col("sum_s_sq")
        nc.scalar.activation(s_sq[:], p_sq[:], ACT.Copy, scale=factor_inv_z_sq[:], accum_out=sum_s_sq[:])

        u = row("u")
        for h in range(2):
            nc.vector.scalar_tensor_tensor(u[:, halves[h]], neg_a[:, halves[h]], beta[:], c0_banks[h][:], ALU.mult, ALU.add)
        t = row("t")
        mean = col("mean")
        nc.vector.scalar_tensor_tensor(t[:], u[:], half_beta[:], s[:], ALU.add, ALU.mult, accum_out=mean[:])
        centred_sq = row("centred_sq")
        nc.scalar.activation(centred_sq[:], u[:], ACT.Square, bias=mean[:], scale=-1.0)
        x = row("x")
        moment = col("moment")
        nc.vector.scalar_tensor_tensor(x[:], u[:], half_beta[:], s_sq[:], ALU.add, ALU.mult, accum_out=moment[:])
        neg_g = col("neg_g")
        nc.vector.tensor_scalar(neg_g[:], sum_s_sq[:], mean[:], moment[:], ALU.mult, ALU.subtract)
        neg_g_mean = col("neg_g_mean")
        nc.scalar.activation(neg_g_mean[:], neg_g[:], ACT.Copy, scale=mean[:])
        y = row("y")
        y_sum = col("y_sum")
        nc.vector.scalar_tensor_tensor(y[:], centred_sq[:], half_beta_sq[:], s_sq[:], ALU.subtract, ALU.mult, accum_out=y_sum[:])
        c = col("c")
        nc.vector.tensor_scalar(c[:], y_sum[:], -1.0, neg_g_mean[:], ALU.mult, ALU.subtract)
        cs = row("cs")
        nc.scalar.activation(cs[:], s[:], ACT.Copy, scale=c[:])
        f = row("f")
        nc.vector.scalar_tensor_tensor(f[:], t[:], neg_g[:], y[:], ALU.mult, ALU.add)
        nc.vector.tensor_tensor(window[:].indirect(offsets[:]), f[:], cs[:], ALU.add)

        result = pool.tile([P, T], F32, name="result")
        start = 0
        for n, width in enumerate(STORE_COLS):
            cols = slice(start, start + width)
            nc.vector.tensor_tensor(result[:, cols], window[:, cols], base_sb[:, cols], ALU.add)
            queue = nc.sync if n % 2 == 0 else nc.scalar
            queue.dma_start(out[:, cols], result[:, cols])
            start = start + width
